import numpy as np
CORES = [0,1,2,3,4,5,6,7]
N = 8
def setup_inputs(rng):
    return {"x1": rng.standard_normal((N, 128, 8), dtype=np.float32), "x2": rng.standard_normal((N, 128, 8), dtype=np.float32)}
def reference(x1, x2):
    out = []
    b = 8 // N
    bl = x1.reshape(N, 128, N, b)
    out.append(np.ascontiguousarray(bl.transpose(2, 1, 0, 3)).reshape(N, 128, 8))
    out.append(np.broadcast_to(x2[4], x2.shape))
    return {"y1": out[0], "y2": out[1]}

from concourse.bass import DstId, RemoteDMATransfer

SCRATCH = {
    "snd": ("sbuf", [128, 8], "float32"),
    "land": ("sbuf", [128, 8], "float32"),
    "bc": ("dram", [128, 8], "float32"),
}
SEMAPHORES = ["ld1", "ld2", "arr1", "arr2", "sent", "st"]

ROOT_RANK = 4
COL_ENGINES = 2
BC_ENGINES = 16


def rank_program(g, core, T, topo):
    rank = T.rank_of(core)
    if rank is None:
        return
    cores = T.cores
    n = len(cores)
    sem = T.sem
    is_root = rank == ROOT_RANK
    others = [j for j in range(n) if j != rank]

    def dst_id(c):
        rid, pid, _se = topo.addr(c)
        return DstId(rid=rid, pnc=pid)

    g.sync.dma_start(T.snd[:], T.x1[:]).then_inc(sem.ld1, 16)
    if is_root:
        g.scalar.dma_start(T.bc[:], T.x2[:]).then_inc(sem.ld2, 16)
        g.scalar.dma_start(T.y2[:], T.x2[:]).then_inc(sem.st, 16)

    g.wait_ge(sem.ld1, 16)
    transfers = []
    for k, j in enumerate(others):
        transfers.append(RemoteDMATransfer(
            dst_ids=[dst_id(cores[j])],
            dma_engine_mask=((1 << COL_ENGINES) - 1) << (COL_ENGINES * k),
            remote_sem=sem.arr1,
            src=T.snd[:, rank_col(j)],
            dst=T.land[:, rank_col(rank)],
        ))
    g.remote_dma_fused(transfers, local_sem=sem.sent)
    sent = COL_ENGINES * len(others)

    if is_root:
        g.wait_ge(sem.ld2, 16)
        g.remote_dma_fused([RemoteDMATransfer(
            dst_ids=[dst_id(cores[j]) for j in others],
            dma_engine_mask=(1 << BC_ENGINES) - 1,
            remote_sem=sem.arr2,
            srcs=[T.bc[:]],
            dsts=[T.bc[:] for _j in others],
        )], local_sem=sem.sent)
        sent += BC_ENGINES

    g.sync.wait_ge(sem.ld1, 16)
    g.sync.dma_start(T.land[:, rank_col(rank)], T.snd[:, rank_col(rank)]).then_inc(sem.arr1, 16)
    g.sync.wait_ge(sem.arr1, 16 + COL_ENGINES * len(others))
    g.sync.dma_start(T.y1[:], T.land[:]).then_inc(sem.st, 16)

    if not is_root:
        g.scalar.wait_ge(sem.arr2, BC_ENGINES)
        g.scalar.dma_start(T.y2[:], T.bc[:]).then_inc(sem.st, 16)

    g.wait_ge(sem.sent, sent)
    g.wait_ge(sem.st, 32)


def rank_col(j):
    return slice(j, j + 1)
